import numpy as np
import ml_dtypes


def mxq(x, axis, fmt="e4m3"):
    dtype, down = {"e4m3": (ml_dtypes.float8_e4m3fn, 7), "e5m2": (ml_dtypes.float8_e5m2, 14)}[fmt]
    v = np.moveaxis(np.asarray(x, np.float32).astype(ml_dtypes.bfloat16).astype(np.float64), axis, -1)
    blocks = v.reshape(v.shape[:-1] + (-1, 32))
    amax = np.abs(blocks).max(-1, keepdims=True)
    byte = np.maximum(np.where(amax > 0, np.frexp(amax)[1] - 1 + 127, 0) - down, 1)
    scale = np.exp2(byte - 127.0)
    codes = (blocks / scale).astype(np.float32).astype(dtype).astype(np.float64)
    return np.moveaxis((codes * scale).reshape(v.shape), -1, axis)


WIDE = False


def mx_kscale(k):
    if not WIDE:
        return np.ones(k)
    levels = np.array([10, -10, 5, -5, 0])
    if k % 512:
        return np.exp2(np.random.permutation(np.resize(levels, k // 32))).repeat(32)
    a = np.empty((k // 512, 16))
    for p in range(k // 512):
        a[p, :8] = np.random.permutation(np.resize(levels, 8))
        for g in range(8):
            far = levels[np.abs(levels - a[p, g]) >= 10]
            a[p, g + 8] = far[np.random.randint(len(far))]
    return np.exp2(a.ravel()).repeat(32)


BF16 = ml_dtypes.bfloat16


def bf(x):
    return np.asarray(x, np.float32).astype(BF16)


def f64(x):
    return np.asarray(x).astype(np.float64)


E2M1 = np.array([0.0, 0.5, 1.0, 1.5, 2.0, 3.0, 4.0, 6.0, -0.0, -0.5, -1.0, -1.5, -2.0, -3.0, -4.0, -6.0])


def pack_weight(w, fmt):
    k, n = w.shape
    w = f64(bf(w)).reshape(k // 32, 32, n)
    amax = np.abs(w).max(1)
    if fmt == "e4m3":
        byte = np.frexp(amax)[1] - 1 + 127 - 7
    else:
        mant, ex = np.frexp(amax / 6.0)
        byte = np.where(mant > 0.5, ex, ex - 1) + 127
    byte = np.clip(np.where(amax > 0, byte, 1), 1, 254)
    scaled = (w * np.exp2(127.0 - byte)[:, None, :]).reshape(k, n).astype(np.float32)
    by_word = np.ascontiguousarray(scaled.reshape(k // 512, 128, 4, n).transpose(0, 1, 3, 2))
    if fmt == "e4m3":
        words = by_word.astype(ml_dtypes.float8_e4m3fn).view(np.uint8)
    else:
        c = by_word.astype(ml_dtypes.float4_e2m1fn).view(np.uint8) & 0xF
        words = c[..., 0::2] | (c[..., 1::2] << 4)
    return np.ascontiguousarray(words), np.ascontiguousarray(byte.astype(np.uint8).reshape(k // 512, 16, n))


def unpack_weight(words, scales, fmt):
    g, p, n, _ = words.shape
    if fmt == "e4m3":
        vals = np.ascontiguousarray(words).view(ml_dtypes.float8_e4m3fn).astype(np.float64)
    else:
        nib = np.empty((g, p, n, 4), np.uint8)
        nib[..., 0::2] = words & 0xF
        nib[..., 1::2] = words >> 4
        vals = E2M1[nib]
    vals = vals * np.repeat(np.exp2(scales.astype(np.float64) - 127.0), 8, axis=1)[..., None]
    return vals.transpose(0, 1, 3, 2).reshape(g * 512, n)
def pack4(w):
    words, scales = pack_weight(w, "e2m1")
    return words.reshape(words.shape[0], 128, -1), scales


def unpack4(words, scales):
    return unpack_weight(words.reshape(words.shape[0], 128, -1, 2), scales, "e2m1")


B, Q, N, D, E = 2, 256, 1024, 512, 512


def gelu_tanh(v):
    return 0.5 * v * (1.0 + np.tanh(np.sqrt(2.0 / np.pi) * (v + 0.044715 * (v * v * v))))


def sigmoid(v):
    return 1.0 / (1.0 + np.exp(-v))


def draw0():
    s1, s2 = mx_kscale(D), mx_kscale(D)
    u = mx_kscale(E)
    t = bf(np.random.standard_normal((B, Q, D)) * s1)
    w1_words, w1_scales = pack4(np.random.standard_normal((D, E)) / np.sqrt(D) / s1[:, None] * u)
    b1 = bf(0.3 * np.random.standard_normal(E) * u)
    f = bf(np.random.standard_normal((B, N, D)) * s2)
    w2_words, w2_scales = pack4(np.random.standard_normal((D, E)) / np.sqrt(D) / s2[:, None])
    b2 = bf(0.3 * np.random.standard_normal(E))
    g = bf((1.0 + 0.1 * np.random.standard_normal(E)) / u)
    return {
        "t": t,
        "w1_words": w1_words,
        "w1_scales": w1_scales,
        "b1": b1,
        "f": f,
        "w2_words": w2_words,
        "w2_scales": w2_scales,
        "b2": b2,
        "g": g,
    }


def core(t, w1_words, w1_scales, b1, f, w2_words, w2_scales, b2, g):
    h = (mxq(f64(t), 2, "e4m3") @ unpack4(w1_words, w1_scales)) + f64(b1)
    v = (mxq(f64(f), 2, "e4m3") @ unpack4(w2_words, w2_scales)) + f64(b2)
    y = f64(g) * gelu_tanh(v)
    scale = 2.0 / np.sqrt(E)
    masks = scale * (mxq(h, 2, "e4m3") @ mxq(y, 2, "e4m3").transpose(0, 2, 1))
    inner = np.sum(sigmoid(4.0 * (masks - 1.0)), axis=-1)
    outer = np.sum(sigmoid(4.0 * (masks + 1.0)), axis=-1)
    stability = inner / outer
    return masks, stability


def e4m3fn_bytes(y):
    return np.clip(np.asarray(y, np.float64), -448.0, 448.0).astype(np.float32).astype(ml_dtypes.float8_e4m3fn).view(np.uint8)


def e4m3fn_values(b):
    return np.asarray(b, np.uint8).view(ml_dtypes.float8_e4m3fn).astype(np.float64)


def setup_inputs():
    d = draw0()
    x0 = np.asarray(d['f']).astype(np.float64)
    s = (np.max(np.abs(x0), axis=(0, 1), keepdims=True) / 448.0).astype(np.float32)
    out = {}
    for k, v in d.items():
        if k == 'f':
            out['f_bytes'] = e4m3fn_bytes(x0 / s.astype(np.float64))
            out['f_scale'] = s
        else:
            out[k] = v
    return out


def reference(t, w1_words, w1_scales, b1, f_bytes, f_scale, w2_words, w2_scales, b2, g):
    return core(t, w1_words, w1_scales, b1, e4m3fn_values(f_bytes) * f_scale.astype(np.float64), w2_words, w2_scales, b2, g)

@@ -1,0 +1,436 @@
+import math
+from contextlib import ExitStack
+
+import concourse.mybir as mybir
+from concourse.masks import make_identity
+
+B, Q, N, D, E = 2, 256, 1024, 512, 512
+FLOPS = 2 * B * Q * D * E + 2 * B * N * D * E + 2 * B * Q * N * E
+
+F32 = mybir.dt.float32
+BF16 = mybir.dt.bfloat16
+I32 = mybir.dt.int32
+U32 = mybir.dt.uint32
+U8 = mybir.dt.uint8
+FP8 = mybir.dt.float8_e4m3fn
+FP8X4 = mybir.dt.float8_e4m3fn_x4
+FP4X4 = mybir.dt.float4_e2m1fn_x4
+ACT = mybir.ActivationFunctionType
+ALU = mybir.AluOpType
+
+P = 128
+PACK = 4
+CHUNK = 512
+CHUNKS = B * N // CHUNK
+QT = B * Q // P
+MASK_SCALE = 2.0 / math.sqrt(E)
+
+
+def tile_hypertokenmaskheadsoftstability_w4_kernel(
+    tc, t, w1_words, w1_scales, b1, f_bytes, f_scale, w2_words, w2_scales, b2, g, out_0, out_1
+):
+    nc = tc.nc
+    with ExitStack() as ctx:
+        sb = ctx.enter_context(tc.tile_pool(name="sb", bufs=1))
+        ps = ctx.enter_context(tc.psum_pool(name="ps", bufs=1))
+        ctx.enter_context(tc.manual_schedule())
+
+        def sbuf(name, shape, dtype):
+            return sb.tile(shape, dtype, name=name, align_bytes=64)
+
+        def bank(index, name, shape=(P, 512), dtype=F32):
+            return ps.tile(list(shape), dtype, name=name, tag="bank%d" % index)
+
+        warm_in = sbuf("warm_in", [P, 16], F32)
+        warm_out = sbuf("warm_out", [P, 16], F32)
+        nc.vector.memset(warm_in[:], 0.0)
+        nc.scalar.activation(out=warm_out[:], in_=warm_in[:], func=ACT.Gelu_apprx_tanh)
+        ident = sbuf("ident", [P, P], F32)
+        make_identity(nc, ident[:])
+
+        raw_scales = [sbuf("raw_scales%d" % w, [P, E], U8) for w in range(2)]
+        for w in range(2):
+            nc.vector.memset(raw_scales[w][:].bitcast(I32), 0)
+        vec_rows = sbuf("vec_rows", [P, P], BF16)
+        nc.vector.memset(vec_rows[:], 0.0)
+
+        f_rows = f_bytes.rearrange("b (c p a) k -> (b c) p (a k)", p=P, a=PACK)
+        fs_cols = sbuf("fs_cols", [P, PACK], F32)
+        nc.sync.dma_start(out=fs_cols[:], in_=f_scale.rearrange("o u (p j) -> p (o u j)", j=PACK))
+        f_raw = [sbuf("f_raw%d" % c, [P, PACK * D], U8) for c in range(CHUNKS)]
+        raw_words = [sbuf("raw_words%d" % w, [P, 2 * E], U8) for w in range(2)]
+        t_raw = [sbuf("t_raw%d" % b, [P, 2, D], BF16) for b in range(B)]
+
+        def load_weight(w, words, scales):
+            nc.sync.dma_start(out=raw_words[w][:].bitcast(I32), in_=words[0].bitcast(I32))
+            for quad in range(4):
+                nc.sync.dma_start(
+                    out=raw_scales[w][32 * quad : 32 * quad + 4, :].bitcast(I32),
+                    in_=scales[0, 4 * quad : 4 * quad + 4, :].bitcast(I32),
+                )
+
+        nc.sync.dma_start(out=f_raw[0][:], in_=f_rows[0])
+        for b in range(B):
+            nc.sync.dma_start(out=t_raw[b][:], in_=t[b].rearrange("(a p) k -> p a k", p=P))
+        load_weight(1, w2_words, w2_scales)
+        nc.sync.dma_start(out=f_raw[1][:], in_=f_rows[1])
+        for v, vec in enumerate((b1, b2, g)):
+            nc.sync.dma_start(
+                out=vec_rows[PACK * v : PACK * (v + 1), :].rearrange("j (q i) -> j q i", i=8),
+                in_=vec.rearrange("(q j i) -> j q i", j=PACK, i=8),
+            )
+        load_weight(0, w1_words, w1_scales)
+        for c in range(2, CHUNKS):
+            nc.sync.dma_start(out=f_raw[c][:], in_=f_rows[c])
+
+        ident_bf = sbuf("ident_bf", [P, P], BF16)
+        nc.vector.tensor_copy(out=ident_bf[:], in_=ident[:])
+        shift = sbuf("shift", [P, 2], F32)
+        nc.vector.memset(shift[:, 0:1], -4.0)
+        nc.vector.memset(shift[:, 1:2], 4.0)
+        stab = sbuf("stab", [P, P], F32)
+        nc.vector.memset(stab[:], 0.0)
+
+        spread_ps = bank(2, "spread_ps")
+        for j in range(PACK):
+            nc.tensor.transpose(
+                spread_ps[:, j * P : (j + 1) * P], fs_cols[:, j : j + 1].to_broadcast([P, P]), ident[:]
+            )
+        fs_spread = sbuf("fs_spread", [P, D], F32)
+        nc.scalar.copy(
+            out=fs_spread[:].rearrange("x (p j) -> x p j", j=PACK),
+            in_=spread_ps[:].rearrange("x (j p) -> x p j", j=PACK),
+        )
+
+        w_codes = [sbuf("w_codes%d" % w, [P, 2 * E], U8) for w in range(2)]
+        w_scales = [sbuf("w_scales%d" % w, [P, E], U8) for w in range(2)]
+
+        def permute_weight(w):
+            nc.vector.tensor_copy(
+                out=w_codes[w][:].bitcast(I32).rearrange("p (j q i) -> p j q i", j=PACK, i=4),
+                in_=raw_words[w][:].bitcast(I32).rearrange("p (q j i) -> p j q i", j=PACK, i=4),
+            )
+            nc.vector.tensor_copy(
+                out=w_scales[w][:].bitcast(I32).rearrange("p (j q i) -> p j q i", j=PACK, i=2),
+                in_=raw_scales[w][:].bitcast(I32).rearrange("p (q j i) -> p j q i", j=PACK, i=2),
+            )
+
+        def weight_slice(w, j):
+            return dict(
+                lhsT=w_codes[w][:, 2 * P * j : 2 * P * (j + 1)].bitcast(FP4X4),
+                lhsT_scale=w_scales[w][:, P * j : P * (j + 1)],
+            )
+
+        def turn(dst, slot, rows):
+            words = rows.bitcast(F32)
+            for u in range(2):
+                col = (2 * slot + u) * P
+                nc.tensor.transpose(dst[:, col : col + P], words[:, u : 2 * P : 2], ident[:])
+
+        def turned_out(grouped, half, src):
+            nc.scalar.copy(
+                out=grouped[:, 1024 * half : 1024 * (half + 1)].bitcast(F32).rearrange("p (a r u) -> p a r u", a=2, u=2),
+                in_=src[:].rearrange("p (a u r) -> p a r u", a=2, u=2),
+            )
+
+        def mx_tiles(name):
+            return sbuf(name + "_codes", [P, 512], U32), sbuf(name + "_scales", [P, 512], U8)
+
+        def quantize(mx, grouped, lo=0, hi=512):
+            codes, scales = mx
+            nc.vector.quantize_mx(
+                out=codes[:, lo:hi].bitcast(FP8X4), scales=scales[:, lo:hi], in_=grouped[:, PACK * lo : PACK * hi]
+            )
+
+        f_wide, f_turned, f_grouped, f_mx, v_ps, gelu, y_grouped, y_mx = {}, {}, {}, {}, {}, {}, {}, {}
+        mask_ps, mask_sb = {}, {}
+
+        def widen(c, a):
+            f_wide[c, a] = sbuf("f_wide%d_%d" % (c, a), [P, D], BF16)
+            nc.vector.tensor_tensor(
+                out=f_wide[c, a][:], in0=f_raw[c][:, a * D : (a + 1) * D].bitcast(FP8), in1=fs_spread[:], op=ALU.mult
+            )
+
+        def f_turn(c, half):
+            f_turned[c, half] = bank(half, "f_turned%d_%d" % (c, half))
+            for slot in range(2):
+                turn(f_turned[c, half], slot, f_wide[c, 2 * half + slot][:])
+
+        def f_out(c, half):
+            if half == 0:
+                f_grouped[c] = sbuf("f_grouped%d" % c, [P, PACK * CHUNK], BF16)
+            turned_out(f_grouped[c], half, f_turned[c, half])
+
+        def f_quantize(c, lo=0, hi=CHUNK):
+            if lo == 0:
+                f_mx[c] = mx_tiles("f%d" % c)
+            quantize(f_mx[c], f_grouped[c], lo, hi)
+
+        def v_matmul(c, j, dst, lo=0, hi=CHUNK):
+            v_ps[c, j, lo] = dst
+            codes, scales = f_mx[c]
+            nc.tensor.matmul_mx(
+                out=dst, rhs=codes[:, lo:hi].bitcast(FP8X4), rhs_scale=scales[:, lo:hi], start=True, stop=True,
+                **weight_slice(1, j)
+            )
+
+        def v_gelu(c, j, lo=0, hi=CHUNK):
+            if j == 0 and lo == 0:
+                gelu[c] = sbuf("gelu%d" % c, [P, PACK, CHUNK], F32)
+            nc.scalar.activation(
+                out=gelu[c][:, j, lo:hi], in_=v_ps[c, j, lo], func=ACT.Gelu_apprx_tanh, bias=vec_cols[:, PACK + j : PACK + j + 1]
+            )
+
+        def y_gain(c, lo=0, hi=CHUNK):
+            if lo == 0:
+                y_grouped[c] = sbuf("y_grouped%d" % c, [P, PACK * CHUNK], BF16)
+            nc.vector.tensor_tensor(
+                out=y_grouped[c][:, PACK * lo : PACK * hi].rearrange("p (c i j) -> p c j i", i=4, j=PACK),
+                in0=gelu[c][:, :, lo:hi].rearrange("p j (c i) -> p c j i", i=4),
+                in1=vec_cols[:, 2 * PACK : 3 * PACK].unsqueeze(1).unsqueeze(3).to_broadcast([P, (hi - lo) // 4, PACK, 4]),
+                op=ALU.mult,
+            )
+
+        def y_quantize(c, lo=0, hi=CHUNK):
+            if lo == 0:
+                y_mx[c] = mx_tiles("y%d" % c)
+            quantize(y_mx[c], y_grouped[c], lo, hi)
+
+        def mask_matmul(c, a, index):
+            mask_ps[c, a] = bank(index, "mask_ps%d_%d" % (c, a))
+            cols = slice((c // 2 * 2 + a) * P, (c // 2 * 2 + a + 1) * P)
+            codes, scales = y_mx[c]
+            nc.tensor.matmul_mx(
+                out=mask_ps[c, a][:], lhsT=h_mx[0][:, cols].bitcast(FP8X4), lhsT_scale=h_mx[1][:, cols],
+                rhs=codes[:].bitcast(FP8X4), rhs_scale=scales[:], start=True, stop=True,
+            )
+
+        def mask_out(c, a, on_vector):
+            qt, half = c // 2 * 2 + a, c % 2
+            if qt not in mask_sb:
+                mask_sb[qt] = sbuf("masks%d" % qt, [P, N], F32)
+            dst = mask_sb[qt][:, half * CHUNK : (half + 1) * CHUNK]
+            src = mask_ps[c, a][:].rearrange("p (a r) -> p r a", a=PACK)
+            if on_vector:
+                nc.vector.tensor_scalar(
+                    out=dst.rearrange("p (r a) -> p r a", a=PACK), in0=src, scalar1=MASK_SCALE, scalar2=None, op0=ALU.mult
+                )
+            else:
+                nc.scalar.activation(out=dst.rearrange("p (r a) -> p r a", a=PACK), in_=src, func=ACT.Copy, scale=MASK_SCALE)
+            nc.sync.dma_start(
+                out=out_0[c // 2, a * P : (a + 1) * P, half * CHUNK : (half + 1) * CHUNK], in_=dst
+            )
+
+        sums = sbuf("sums", [P, 2, QT, 2], F32)
+
+        def sigmoid_sum(side, qt, part, src, scale, width):
+            junk = sbuf("junk%d_%d_%d" % (side, qt, part), [P, width], BF16)
+            nc.scalar.activation(
+                out=junk[:], in_=src, func=ACT.Sigmoid, scale=scale, bias=shift[:, side : side + 1],
+                accum_out=sums[:, side, qt, part : part + 1],
+            )
+
+        t_grouped = sbuf("t_grouped", [P, PACK * 512], BF16)
+        h_grouped = sbuf("h_grouped", [P, PACK * 512], BF16)
+        t_mx, h_mx = mx_tiles("t"), mx_tiles("h")
+        vec_cols = sbuf("vec_cols", [P, 3 * PACK], F32)
+        t_turned, h_ps = {}, {}
+
+        def t_turn(half):
+            t_turned[half] = bank(6 + half, "t_turned%d" % half)
+            for slot in range(2):
+                turn(t_turned[half], slot, t_raw[half][:, slot, :])
+
+        def h_matmul(qt):
+            h_ps[qt] = bank(6 + qt % 2, "h_ps%d" % qt)
+            cols = slice(qt * P, (qt + 1) * P)
+            for j in range(PACK):
+                nc.tensor.matmul_mx(
+                    out=h_ps[qt][:, j * P : (j + 1) * P], rhs=t_mx[0][:, cols].bitcast(FP8X4), rhs_scale=t_mx[1][:, cols],
+                    start=True, stop=True, **weight_slice(0, j)
+                )
+
+        def h_out(qt):
+            nc.vector.tensor_tensor(
+                out=h_grouped[:, 512 * qt : 512 * (qt + 1)].rearrange("p (r j) -> p r j", j=PACK),
+                in0=h_ps[qt][:].rearrange("p (j r) -> p r j", j=PACK),
+                in1=vec_cols[:, 0:PACK].unsqueeze(1).to_broadcast([P, P, PACK]),
+                op=ALU.add,
+            )
+
+        def ps_sigmoids(c, a, sides=(1, 0)):
+            for side in sides:
+                sigmoid_sum(side, c // 2 * 2 + a, c % 2, mask_ps[c, a][:], 4.0 * MASK_SCALE, CHUNK)
+
+        outer = sbuf("outer", [P, QT], F32)
+        recip = sbuf("recip", [P, QT], F32)
+
+        def outer_recip(lo, hi):
+            nc.vector.tensor_tensor(out=outer[:, lo:hi], in0=sums[:, 1, lo:hi, 0], in1=sums[:, 1, lo:hi, 1], op=ALU.add)
+            nc.vector.reciprocal(out=recip[:, lo:hi], in_=outer[:, lo:hi])
+
+        def ratio(qt):
+            nc.vector.scalar_tensor_tensor(
+                out=stab[:, 32 * qt : 32 * qt + 1], in0=sums[:, 0, qt, 0:1], scalar=sums[:, 0, qt, 1:2],
+                in1=recip[:, qt : qt + 1], op0=ALU.add, op1=ALU.mult,
+            )
+
+        first = {}
+
+        def first_matmul(h, j):
+            if j % 2 == 0:
+                first[h, j // 2] = bank(2 + 2 * h + j // 2, "first%d_%d" % (h, j))
+            v_matmul(0, j, first[h, j // 2][:, 256 * (j % 2) : 256 * (j % 2 + 1)], 256 * h, 256 * h + 256)
+
+        widen(0, 0)
+        widen(0, 1)
+        widen(0, 2)
+        widen(0, 3)
+        permute_weight(1)
+        widen(1, 0)
+        t_turn(0)
+        t_turn(1)
+        f_turn(0, 0)
+        f_turn(0, 1)
+        vec_ps = bank(5, "vec_ps", (P, P), BF16)
+        nc.tensor.transpose(vec_ps[:], vec_rows[:], ident_bf[:])
+        turned_out(t_grouped, 0, t_turned[0])
+        turned_out(t_grouped, 1, t_turned[1])
+        f_out(0, 0)
+        f_out(0, 1)
+        nc.scalar.copy(out=vec_cols[:], in_=vec_ps[:, 0 : 3 * PACK])
+        f_quantize(0, 0, 256)
+        widen(1, 1)
+        widen(1, 2)
+        f_quantize(0, 256, 512)
+        widen(1, 3)
+        widen(2, 0)
+        widen(2, 1)
+        widen(2, 2)
+        widen(2, 3)
+        widen(3, 0)
+        first_matmul(0, 0)
+        first_matmul(0, 1)
+        first_matmul(0, 2)
+        first_matmul(0, 3)
+        f_turn(1, 0)
+        first_matmul(1, 0)
+        first_matmul(1, 1)
+        f_turn(1, 1)
+        first_matmul(1, 2)
+        first_matmul(1, 3)
+        v_gelu(0, 0, 0, 256)
+        v_gelu(0, 1, 0, 256)
+        v_gelu(0, 2, 0, 256)
+        v_gelu(0, 3, 0, 256)
+        f_out(1, 0)
+        v_gelu(0, 0, 256, 512)
+        f_out(1, 1)
+        v_gelu(0, 1, 256, 512)
+        v_gelu(0, 2, 256, 512)
+        v_gelu(0, 3, 256, 512)
+        f_turn(2, 0)
+        f_turn(2, 1)
+        f_quantize(1)
+        widen(3, 1)
+        widen(3, 2)
+        widen(3, 3)
+        quantize(t_mx, t_grouped)
+        permute_weight(0)
+        f_out(2, 0)
+        f_out(2, 1)
+        v_matmul(1, 0, bank(2, "v_ps1_0")[:])
+        v_matmul(1, 1, bank(3, "v_ps1_1")[:])
+        f_turn(3, 0)
+        v_matmul(1, 2, bank(4, "v_ps1_2")[:])
+        v_matmul(1, 3, bank(5, "v_ps1_3")[:])
+        f_turn(3, 1)
+        h_matmul(0)
+        h_matmul(1)
+        f_quantize(2)
+        y_gain(0, 0, 256)
+        v_gelu(1, 0)
+        v_gelu(1, 1)
+        f_out(3, 0)
+        v_gelu(1, 2)
+        f_out(3, 1)
+        v_gelu(1, 3)
+        v_matmul(2, 0, bank(2, "v_ps2_0")[:])
+        v_matmul(2, 1, bank(3, "v_ps2_1")[:])
+        v_matmul(2, 2, bank(4, "v_ps2_2")[:])
+        v_matmul(2, 3, bank(5, "v_ps2_3")[:])
+        f_quantize(3)
+        y_gain(0, 256, 512)
+        h_out(0)
+        y_quantize(0)
+        h_out(1)
+        y_gain(1, 0, 256)
+        quantize(h_mx, h_grouped, 0, 256)
+        y_gain(1, 256, 512)
+        v_gelu(2, 0)
+        v_gelu(2, 1)
+        v_gelu(2, 2)
+        v_gelu(2, 3)
+        v_matmul(3, 0, bank(2, "v_ps3_0")[:])
+        v_matmul(3, 1, bank(3, "v_ps3_1")[:])
+        v_matmul(3, 2, bank(4, "v_ps3_2")[:])
+        v_matmul(3, 3, bank(5, "v_ps3_3")[:])
+        h_matmul(2)
+        mask_matmul(0, 0, 0)
+        mask_matmul(0, 1, 1)
+        h_matmul(3)
+        h_out(2)
+        y_quantize(1)
+        h_out(3)
+        y_gain(2)
+        quantize(h_mx, h_grouped, 256, 512)
+        y_quantize(2)
+        v_gelu(3, 0)
+        v_gelu(3, 1)
+        v_gelu(3, 2)
+        v_gelu(3, 3)
+        ps_sigmoids(0, 0, (1,))
+        ps_sigmoids(0, 0, (0,))
+        ps_sigmoids(0, 1, (1,))
+        ps_sigmoids(0, 1, (0,))
+        mask_out(0, 0, False)
+        mask_out(0, 1, False)
+        mask_matmul(1, 0, 2)
+        mask_matmul(1, 1, 3)
+        mask_matmul(2, 0, 4)
+        mask_matmul(2, 1, 5)
+        y_gain(3)
+        ps_sigmoids(1, 0, (1,))
+        ps_sigmoids(1, 0, (0,))
+        ps_sigmoids(1, 1, (1,))
+        ps_sigmoids(1, 1, (0,))
+        ps_sigmoids(2, 0, (1,))
+        ps_sigmoids(2, 0, (0,))
+        ps_sigmoids(2, 1, (1,))
+        ps_sigmoids(2, 1, (0,))
+        mask_out(1, 0, True)
+        y_quantize(3)
+        mask_out(1, 1, True)
+        outer_recip(0, 2)
+        mask_out(2, 0, True)
+        ratio(0)
+        ratio(1)
+        mask_matmul(3, 0, 6)
+        mask_matmul(3, 1, 7)
+        mask_out(3, 1, True)
+        mask_out(2, 1, True)
+        ps_sigmoids(3, 0, (1,))
+        ps_sigmoids(3, 0, (0,))
+        ps_sigmoids(3, 1, (1,))
+        ps_sigmoids(3, 1, (0,))
+        mask_out(3, 0, True)
+        outer_recip(2, 4)
+        ratio(2)
+        ratio(3)
+
+        stab_turned = sbuf("stab_turned", [P, P], F32)
+        nc.vector.transpose(out=stab_turned[:], in_=stab[:])
+        nc.sync.dma_start(
+            out=out_1.rearrange("b (a s i) -> s (b a) i", a=2, i=32),
+            in_=stab_turned[0:P:32, :].rearrange("s (j i) -> s j i", i=32),
+        )

@@ -20,10 +20,16 @@ ALU = mybir.AluOpType
 
 P = 128
 PACK = 4
+BANK = 512
 CHUNK = 512
+HALF = CHUNK // 2
 CHUNKS = B * N // CHUNK
-QT = B * Q // P
+TILES = B * Q // P
+RUN = 4
 MASK_SCALE = 2.0 / math.sqrt(E)
+W1, W2 = 0, 1
+BIAS1, BIAS2, GAIN = 0, 1, 2
+INNER, OUTER = 0, 1
 
 
 def tile_hypertokenmaskheadsoftstability_w4_kernel(
@@ -35,11 +41,11 @@ def tile_hypertokenmaskheadsoftstability_w4_kernel(
         ps = ctx.enter_context(tc.psum_pool(name="ps", bufs=1))
         ctx.enter_context(tc.manual_schedule())
 
-        def sbuf(name, shape, dtype):
-            return sb.tile(shape, dtype, name=name, align_bytes=64)
+        def sbuf(name, shape, dtype, tag=None):
+            return sb.tile(shape, dtype, name=name, tag=tag or name, align_bytes=64)
 
-        def bank(index, name, shape=(P, 512), dtype=F32):
-            return ps.tile(list(shape), dtype, name=name, tag="bank%d" % index)
+        def bank(index, name, width=BANK, dtype=F32):
+            return ps.tile([P, width], dtype, name=name, tag="bank%d" % index)
 
         warm_in = sbuf("warm_in", [P, 16], F32)
         warm_out = sbuf("warm_out", [P, 16], F32)
@@ -48,18 +54,17 @@ def tile_hypertokenmaskheadsoftstability_w4_kernel(
         ident = sbuf("ident", [P, P], F32)
         make_identity(nc, ident[:])
 
-        raw_scales = [sbuf("raw_scales%d" % w, [P, E], U8) for w in range(2)]
-        for w in range(2):
+        raw_scales = [sbuf("raw_scales%d" % w, [P, E], U8) for w in (W1, W2)]
+        for w in (W1, W2):
             nc.vector.memset(raw_scales[w][:].bitcast(I32), 0)
         vec_rows = sbuf("vec_rows", [P, P], BF16)
         nc.vector.memset(vec_rows[:], 0.0)
 
-        f_rows = f_bytes.rearrange("b (c p a) k -> (b c) p (a k)", p=P, a=PACK)
+        f_rows = f_bytes.rearrange("b (c r a) k -> (b c) r (a k)", r=P, a=PACK)
         fs_cols = sbuf("fs_cols", [P, PACK], F32)
-        nc.sync.dma_start(out=fs_cols[:], in_=f_scale.rearrange("o u (p j) -> p (o u j)", j=PACK))
         f_raw = [sbuf("f_raw%d" % c, [P, PACK * D], U8) for c in range(CHUNKS)]
-        raw_words = [sbuf("raw_words%d" % w, [P, 2 * E], U8) for w in range(2)]
         t_raw = [sbuf("t_raw%d" % b, [P, 2, D], BF16) for b in range(B)]
+        raw_words = [sbuf("raw_words%d" % w, [P, 2 * E], U8) for w in (W1, W2)]
 
         def load_weight(w, words, scales):
             nc.sync.dma_start(out=raw_words[w][:].bitcast(I32), in_=words[0].bitcast(I32))
@@ -69,51 +74,47 @@ def tile_hypertokenmaskheadsoftstability_w4_kernel(
                     in_=scales[0, 4 * quad : 4 * quad + 4, :].bitcast(I32),
                 )
 
+        nc.sync.dma_start(out=fs_cols[:], in_=f_scale.rearrange("o u (p j) -> p (o u j)", j=PACK))
         nc.sync.dma_start(out=f_raw[0][:], in_=f_rows[0])
         for b in range(B):
             nc.sync.dma_start(out=t_raw[b][:], in_=t[b].rearrange("(a p) k -> p a k", p=P))
-        load_weight(1, w2_words, w2_scales)
+        load_weight(W2, w2_words, w2_scales)
         nc.sync.dma_start(out=f_raw[1][:], in_=f_rows[1])
         for v, vec in enumerate((b1, b2, g)):
             nc.sync.dma_start(
                 out=vec_rows[PACK * v : PACK * (v + 1), :].rearrange("j (q i) -> j q i", i=8),
                 in_=vec.rearrange("(q j i) -> j q i", j=PACK, i=8),
             )
-        load_weight(0, w1_words, w1_scales)
+        load_weight(W1, w1_words, w1_scales)
         for c in range(2, CHUNKS):
             nc.sync.dma_start(out=f_raw[c][:], in_=f_rows[c])
 
         ident_bf = sbuf("ident_bf", [P, P], BF16)
         nc.vector.tensor_copy(out=ident_bf[:], in_=ident[:])
         shift = sbuf("shift", [P, 2], F32)
-        nc.vector.memset(shift[:, 0:1], -4.0)
-        nc.vector.memset(shift[:, 1:2], 4.0)
+        nc.vector.memset(shift[:, INNER : INNER + 1], -4.0)
+        nc.vector.memset(shift[:, OUTER : OUTER + 1], 4.0)
         stab = sbuf("stab", [P, P], F32)
         nc.vector.memset(stab[:], 0.0)
 
         spread_ps = bank(2, "spread_ps")
         for j in range(PACK):
-            nc.tensor.transpose(
-                spread_ps[:, j * P : (j + 1) * P], fs_cols[:, j : j + 1].to_broadcast([P, P]), ident[:]
-            )
+            nc.tensor.transpose(spread_ps[:, j * P : (j + 1) * P], fs_cols[:, j : j + 1].to_broadcast([P, P]), ident[:])
         fs_spread = sbuf("fs_spread", [P, D], F32)
         nc.scalar.copy(
             out=fs_spread[:].rearrange("x (p j) -> x p j", j=PACK),
             in_=spread_ps[:].rearrange("x (j p) -> x p j", j=PACK),
         )
 
-        w_codes = [sbuf("w_codes%d" % w, [P, 2 * E], U8) for w in range(2)]
-        w_scales = [sbuf("w_scales%d" % w, [P, E], U8) for w in range(2)]
+        w_codes = [sbuf("w_codes%d" % w, [P, 2 * E], U8) for w in (W1, W2)]
+        w_scales = [sbuf("w_scales%d" % w, [P, E], U8) for w in (W1, W2)]
 
         def permute_weight(w):
-            nc.vector.tensor_copy(
-                out=w_codes[w][:].bitcast(I32).rearrange("p (j q i) -> p j q i", j=PACK, i=4),
-                in_=raw_words[w][:].bitcast(I32).rearrange("p (q j i) -> p j q i", j=PACK, i=4),
-            )
-            nc.vector.tensor_copy(
-                out=w_scales[w][:].bitcast(I32).rearrange("p (j q i) -> p j q i", j=PACK, i=2),
-                in_=raw_scales[w][:].bitcast(I32).rearrange("p (q j i) -> p j q i", j=PACK, i=2),
-            )
+            for dst, src, words in ((w_codes, raw_words, 4), (w_scales, raw_scales, 2)):
+                nc.vector.tensor_copy(
+                    out=dst[w][:].bitcast(I32).rearrange("p (j q i) -> p j q i", j=PACK, i=words),
+                    in_=src[w][:].bitcast(I32).rearrange("p (q j i) -> p j q i", j=PACK, i=words),
+                )
 
         def weight_slice(w, j):
             return dict(
@@ -121,310 +122,280 @@ def tile_hypertokenmaskheadsoftstability_w4_kernel(
                 lhsT_scale=w_scales[w][:, P * j : P * (j + 1)],
             )
 
-        def turn(dst, slot, rows):
-            words = rows.bitcast(F32)
-            for u in range(2):
-                col = (2 * slot + u) * P
-                nc.tensor.transpose(dst[:, col : col + P], words[:, u : 2 * P : 2], ident[:])
+        def mx_tiles(name):
+            return sbuf(name + "_codes", [P, CHUNK], U32), sbuf(name + "_scales", [P, CHUNK], U8)
+
+        def quantize(mx, lo, hi, grouped):
+            nc.vector.quantize_mx(out=mx[0][:, lo:hi].bitcast(FP8X4), scales=mx[1][:, lo:hi], in_=grouped)
+
+        def turn(index, name, rows):
+            dst = bank(index, name)
+            for slot in range(2):
+                words = rows[slot].bitcast(F32)
+                for u in range(2):
+                    col = (2 * slot + u) * P
+                    nc.tensor.transpose(dst[:, col : col + P], words[:, u : 2 * P : 2], ident[:])
+            return dst
 
         def turned_out(grouped, half, src):
+            words = grouped[:, PACK * HALF * half : PACK * HALF * (half + 1)].bitcast(F32)
             nc.scalar.copy(
-                out=grouped[:, 1024 * half : 1024 * (half + 1)].bitcast(F32).rearrange("p (a r u) -> p a r u", a=2, u=2),
+                out=words.rearrange("p (a r u) -> p a r u", a=2, u=2),
                 in_=src[:].rearrange("p (a u r) -> p a r u", a=2, u=2),
             )
 
-        def mx_tiles(name):
-            return sbuf(name + "_codes", [P, 512], U32), sbuf(name + "_scales", [P, 512], U8)
-
-        def quantize(mx, grouped, lo=0, hi=512):
-            codes, scales = mx
-            nc.vector.quantize_mx(
-                out=codes[:, lo:hi].bitcast(FP8X4), scales=scales[:, lo:hi], in_=grouped[:, PACK * lo : PACK * hi]
-            )
-
-        f_wide, f_turned, f_grouped, f_mx, v_ps, gelu, y_grouped, y_mx = {}, {}, {}, {}, {}, {}, {}, {}
-        mask_ps, mask_sb = {}, {}
+        vec_cols = sbuf("vec_cols", [P, 3 * PACK], F32)
+        f_wide = [[sbuf("f_wide%d_%d" % (c, a), [P, D], BF16) for a in range(PACK)] for c in range(CHUNKS)]
+        f_grouped = [
+            sbuf("f_grouped%d" % c, [P, PACK * CHUNK], BF16, "side0" if c == CHUNKS - 1 else None) for c in range(CHUNKS)
+        ]
+        t_grouped = sbuf("t_grouped", [P, PACK * B * Q], BF16)
+        h_grouped = [sbuf("h_grouped%d" % b, [P, PACK * Q], BF16, "side1" if b == 0 else None) for b in range(B)]
+        gelu = [sbuf("gelu%d" % c, [P, PACK, CHUNK], F32) for c in range(CHUNKS)]
+        y_grouped = {c: sbuf("y_grouped%d" % c, [P, PACK * CHUNK], BF16) for c in (0, 2, 3)}
+        f_mx = [mx_tiles("f%d" % c) for c in range(CHUNKS)]
+        y_mx = [mx_tiles("y%d" % c) for c in range(CHUNKS)]
+        t_mx, h_mx = mx_tiles("t"), mx_tiles("h")
+        mask_sb = [sbuf("mask_sb%d" % tile, [P, N], F32) for tile in range(TILES)]
+        sums = sbuf("sums", [P, 2, TILES, 2], F32)
+        outer = sbuf("outer", [P, TILES], F32)
+        recip = sbuf("recip", [P, TILES], F32)
+        f_turned, v_ps, h_ps, mask_ps, y_side = {}, {}, {}, {}, {}
 
         def widen(c, a):
-            f_wide[c, a] = sbuf("f_wide%d_%d" % (c, a), [P, D], BF16)
             nc.vector.tensor_tensor(
-                out=f_wide[c, a][:], in0=f_raw[c][:, a * D : (a + 1) * D].bitcast(FP8), in1=fs_spread[:], op=ALU.mult
+                out=f_wide[c][a][:], in0=f_raw[c][:, a * D : (a + 1) * D].bitcast(FP8), in1=fs_spread[:], op=ALU.mult
             )
 
         def f_turn(c, half):
-            f_turned[c, half] = bank(half, "f_turned%d_%d" % (c, half))
-            for slot in range(2):
-                turn(f_turned[c, half], slot, f_wide[c, 2 * half + slot][:])
+            rows = [f_wide[c][2 * half + slot][:] for slot in range(2)]
+            f_turned[c, half] = turn(half, "f_turned%d_%d" % (c, half), rows)
 
         def f_out(c, half):
-            if half == 0:
-                f_grouped[c] = sbuf("f_grouped%d" % c, [P, PACK * CHUNK], BF16)
             turned_out(f_grouped[c], half, f_turned[c, half])
 
         def f_quantize(c, lo=0, hi=CHUNK):
-            if lo == 0:
-                f_mx[c] = mx_tiles("f%d" % c)
-            quantize(f_mx[c], f_grouped[c], lo, hi)
+            quantize(f_mx[c], lo, hi, f_grouped[c][:, PACK * lo : PACK * hi])
 
         def v_matmul(c, j, dst, lo=0, hi=CHUNK):
             v_ps[c, j, lo] = dst
-            codes, scales = f_mx[c]
             nc.tensor.matmul_mx(
-                out=dst, rhs=codes[:, lo:hi].bitcast(FP8X4), rhs_scale=scales[:, lo:hi], start=True, stop=True,
-                **weight_slice(1, j)
+                out=dst, rhs=f_mx[c][0][:, lo:hi].bitcast(FP8X4), rhs_scale=f_mx[c][1][:, lo:hi],
+                start=True, stop=True, **weight_slice(W2, j)
             )
+
+        def v_whole(c, j):
+            v_matmul(c, j, bank(2 + j, "v_ps%d_%d" % (c, j))[:])
+
+        def v_first_pair(half, pair):
+            dst = bank(2 + 2 * half + pair, "v_first%d_%d" % (half, pair))
+            for slot in range(2):
+                v_matmul(0, 2 * pair + slot, dst[:, HALF * slot : HALF * (slot + 1)], HALF * half, HALF * (half + 1))
 
         def v_gelu(c, j, lo=0, hi=CHUNK):
-            if j == 0 and lo == 0:
-                gelu[c] = sbuf("gelu%d" % c, [P, PACK, CHUNK], F32)
+            col = PACK * BIAS2 + j
             nc.scalar.activation(
-                out=gelu[c][:, j, lo:hi], in_=v_ps[c, j, lo], func=ACT.Gelu_apprx_tanh, bias=vec_cols[:, PACK + j : PACK + j + 1]
+                out=gelu[c][:, j, lo:hi], in_=v_ps[c, j, lo], func=ACT.Gelu_apprx_tanh, bias=vec_cols[:, col : col + 1]
             )
 
-        def y_gain(c, lo=0, hi=CHUNK):
-            if lo == 0:
-                y_grouped[c] = sbuf("y_grouped%d" % c, [P, PACK * CHUNK], BF16)
-            nc.vector.tensor_tensor(
-                out=y_grouped[c][:, PACK * lo : PACK * hi].rearrange("p (c i j) -> p c j i", i=4, j=PACK),
-                in0=gelu[c][:, :, lo:hi].rearrange("p j (c i) -> p c j i", i=4),
-                in1=vec_cols[:, 2 * PACK : 3 * PACK].unsqueeze(1).unsqueeze(3).to_broadcast([P, (hi - lo) // 4, PACK, 4]),
+        def gain(engine, dst, c, lo, hi, cols):
+            gains = cols[:, PACK * GAIN : PACK * (GAIN + 1)].unsqueeze(1).unsqueeze(3)
+            engine.tensor_tensor(
+                out=dst.rearrange("p (c i j) -> p c j i", i=RUN, j=PACK),
+                in0=gelu[c][:, :, lo:hi].rearrange("p j (c i) -> p c j i", i=RUN),
+                in1=gains.to_broadcast([P, (hi - lo) // RUN, PACK, RUN]),
                 op=ALU.mult,
             )
 
-        def y_quantize(c, lo=0, hi=CHUNK):
-            if lo == 0:
-                y_mx[c] = mx_tiles("y%d" % c)
-            quantize(y_mx[c], y_grouped[c], lo, hi)
+        def y_gain(c, cols, lo=0, hi=CHUNK):
+            gain(nc.vector, y_grouped[c][:, PACK * lo : PACK * hi], c, lo, hi, cols)
 
-        def mask_matmul(c, a, index):
-            mask_ps[c, a] = bank(index, "mask_ps%d_%d" % (c, a))
-            cols = slice((c // 2 * 2 + a) * P, (c // 2 * 2 + a + 1) * P)
-            codes, scales = y_mx[c]
-            nc.tensor.matmul_mx(
-                out=mask_ps[c, a][:], lhsT=h_mx[0][:, cols].bitcast(FP8X4), lhsT_scale=h_mx[1][:, cols],
-                rhs=codes[:].bitcast(FP8X4), rhs_scale=scales[:], start=True, stop=True,
-            )
+        def y_quantize(c):
+            quantize(y_mx[c], 0, CHUNK, y_grouped[c][:])
 
-        def mask_out(c, a, on_vector):
-            qt, half = c // 2 * 2 + a, c % 2
-            if qt not in mask_sb:
-                mask_sb[qt] = sbuf("masks%d" % qt, [P, N], F32)
-            dst = mask_sb[qt][:, half * CHUNK : (half + 1) * CHUNK]
-            src = mask_ps[c, a][:].rearrange("p (a r) -> p r a", a=PACK)
-            if on_vector:
-                nc.vector.tensor_scalar(
-                    out=dst.rearrange("p (r a) -> p r a", a=PACK), in0=src, scalar1=MASK_SCALE, scalar2=None, op0=ALU.mult
-                )
-            else:
-                nc.scalar.activation(out=dst.rearrange("p (r a) -> p r a", a=PACK), in_=src, func=ACT.Copy, scale=MASK_SCALE)
-            nc.sync.dma_start(
-                out=out_0[c // 2, a * P : (a + 1) * P, half * CHUNK : (half + 1) * CHUNK], in_=dst
-            )
+        def side_gain(half):
+            y_side[half] = sbuf("y_side%d" % half, [P, PACK * HALF], BF16, "side%d" % half)
+            gain(nc.gpsimd, y_side[half][:], 1, HALF * half, HALF * (half + 1), vec_cols)
 
-        sums = sbuf("sums", [P, 2, QT, 2], F32)
+        def side_quantize(half):
+            quantize(y_mx[1], HALF * half, HALF * (half + 1), y_side[half][:])
 
-        def sigmoid_sum(side, qt, part, src, scale, width):
-            junk = sbuf("junk%d_%d_%d" % (side, qt, part), [P, width], BF16)
-            nc.scalar.activation(
-                out=junk[:], in_=src, func=ACT.Sigmoid, scale=scale, bias=shift[:, side : side + 1],
-                accum_out=sums[:, side, qt, part : part + 1],
-            )
-
-        t_grouped = sbuf("t_grouped", [P, PACK * 512], BF16)
-        h_grouped = sbuf("h_grouped", [P, PACK * 512], BF16)
-        t_mx, h_mx = mx_tiles("t"), mx_tiles("h")
-        vec_cols = sbuf("vec_cols", [P, 3 * PACK], F32)
-        t_turned, h_ps = {}, {}
-
-        def t_turn(half):
-            t_turned[half] = bank(6 + half, "t_turned%d" % half)
-            for slot in range(2):
-                turn(t_turned[half], slot, t_raw[half][:, slot, :])
-
-        def h_matmul(qt):
-            h_ps[qt] = bank(6 + qt % 2, "h_ps%d" % qt)
-            cols = slice(qt * P, (qt + 1) * P)
+        def h_matmul(tile):
+            h_ps[tile] = bank(6 + tile % 2, "h_ps%d" % tile)
+            cols = slice(tile * P, (tile + 1) * P)
             for j in range(PACK):
                 nc.tensor.matmul_mx(
-                    out=h_ps[qt][:, j * P : (j + 1) * P], rhs=t_mx[0][:, cols].bitcast(FP8X4), rhs_scale=t_mx[1][:, cols],
-                    start=True, stop=True, **weight_slice(0, j)
+                    out=h_ps[tile][:, j * P : (j + 1) * P], rhs=t_mx[0][:, cols].bitcast(FP8X4), rhs_scale=t_mx[1][:, cols],
+                    start=True, stop=True, **weight_slice(W1, j)
                 )
 
-        def h_out(qt):
+        def h_out(tile):
+            lo = PACK * P * (tile % 2)
             nc.vector.tensor_tensor(
-                out=h_grouped[:, 512 * qt : 512 * (qt + 1)].rearrange("p (r j) -> p r j", j=PACK),
-                in0=h_ps[qt][:].rearrange("p (j r) -> p r j", j=PACK),
-                in1=vec_cols[:, 0:PACK].unsqueeze(1).to_broadcast([P, P, PACK]),
+                out=h_grouped[tile // 2][:, lo : lo + PACK * P].rearrange("p (r j) -> p r j", j=PACK),
+                in0=h_ps[tile][:].rearrange("p (j r) -> p r j", j=PACK),
+                in1=vec_cols[:, PACK * BIAS1 : PACK * (BIAS1 + 1)].unsqueeze(1).to_broadcast([P, P, PACK]),
                 op=ALU.add,
             )
 
-        def ps_sigmoids(c, a, sides=(1, 0)):
-            for side in sides:
-                sigmoid_sum(side, c // 2 * 2 + a, c % 2, mask_ps[c, a][:], 4.0 * MASK_SCALE, CHUNK)
+        def h_quantize(b):
+            quantize(h_mx, Q * b, Q * (b + 1), h_grouped[b][:])
 
-        outer = sbuf("outer", [P, QT], F32)
-        recip = sbuf("recip", [P, QT], F32)
-
-        def outer_recip(lo, hi):
-            nc.vector.tensor_tensor(out=outer[:, lo:hi], in0=sums[:, 1, lo:hi, 0], in1=sums[:, 1, lo:hi, 1], op=ALU.add)
-            nc.vector.reciprocal(out=recip[:, lo:hi], in_=outer[:, lo:hi])
-
-        def ratio(qt):
-            nc.vector.scalar_tensor_tensor(
-                out=stab[:, 32 * qt : 32 * qt + 1], in0=sums[:, 0, qt, 0:1], scalar=sums[:, 0, qt, 1:2],
-                in1=recip[:, qt : qt + 1], op0=ALU.add, op1=ALU.mult,
+        def mask_matmul(c, a, index):
+            mask_ps[c, a] = bank(index, "mask_ps%d_%d" % (c, a))
+            tile = c // 2 * 2 + a
+            cols = slice(tile * P, (tile + 1) * P)
+            nc.tensor.matmul_mx(
+                out=mask_ps[c, a][:], lhsT=h_mx[0][:, cols].bitcast(FP8X4), lhsT_scale=h_mx[1][:, cols],
+                rhs=y_mx[c][0][:].bitcast(FP8X4), rhs_scale=y_mx[c][1][:], start=True, stop=True,
             )
 
-        first = {}
+        def mask_out(c, a, on_scalar=False):
+            cols = slice(c % 2 * CHUNK, (c % 2 + 1) * CHUNK)
+            rows = mask_sb[c // 2 * 2 + a][:, cols]
+            dst = rows.rearrange("p (r a) -> p r a", a=PACK)
+            src = mask_ps[c, a][:].rearrange("p (a r) -> p r a", a=PACK)
+            if on_scalar:
+                nc.scalar.activation(out=dst, in_=src, func=ACT.Copy, scale=MASK_SCALE)
+            else:
+                nc.vector.tensor_scalar(out=dst, in0=src, scalar1=MASK_SCALE, scalar2=None, op0=ALU.mult)
+            nc.sync.dma_start(out=out_0[c // 2, a * P : (a + 1) * P, cols], in_=rows)
 
-        def first_matmul(h, j):
-            if j % 2 == 0:
-                first[h, j // 2] = bank(2 + 2 * h + j // 2, "first%d_%d" % (h, j))
-            v_matmul(0, j, first[h, j // 2][:, 256 * (j % 2) : 256 * (j % 2 + 1)], 256 * h, 256 * h + 256)
+        def sigmoid_sums(c, a):
+            tile = c // 2 * 2 + a
+            for side in (OUTER, INNER):
+                values = sbuf("sigmoid%d_%d_%d" % (c, a, side), [P, CHUNK], BF16)
+                nc.scalar.activation(
+                    out=values[:], in_=mask_ps[c, a][:], func=ACT.Sigmoid, scale=4.0 * MASK_SCALE,
+                    bias=shift[:, side : side + 1], accum_out=sums[:, side, tile, c % 2 : c % 2 + 1],
+                )
 
-        widen(0, 0)
-        widen(0, 1)
-        widen(0, 2)
-        widen(0, 3)
-        permute_weight(1)
-        widen(1, 0)
-        t_turn(0)
-        t_turn(1)
-        f_turn(0, 0)
-        f_turn(0, 1)
-        vec_ps = bank(5, "vec_ps", (P, P), BF16)
+        def outer_recip(b):
+            tiles = slice(2 * b, 2 * b + 2)
+            nc.vector.tensor_tensor(out=outer[:, tiles], in0=sums[:, OUTER, tiles, 0], in1=sums[:, OUTER, tiles, 1], op=ALU.add)
+            nc.vector.reciprocal(out=recip[:, tiles], in_=outer[:, tiles])
+
+        def ratio(tile):
+            nc.vector.scalar_tensor_tensor(
+                out=stab[:, 32 * tile : 32 * tile + 1], in0=sums[:, INNER, tile, 0:1], scalar=sums[:, INNER, tile, 1:2],
+                in1=recip[:, tile : tile + 1], op0=ALU.add, op1=ALU.mult,
+            )
+
+        for a in range(PACK):
+            widen(0, a)
+        for b in range(B):
+            turned_out(t_grouped, b, turn(6 + b, "t_turned%d" % b, [t_raw[b][:, slot, :] for slot in range(2)]))
+        for half in range(2):
+            f_turn(0, half)
+            f_out(0, half)
+        vec_ps = bank(5, "vec_ps", P, BF16)
         nc.tensor.transpose(vec_ps[:], vec_rows[:], ident_bf[:])
-        turned_out(t_grouped, 0, t_turned[0])
-        turned_out(t_grouped, 1, t_turned[1])
-        f_out(0, 0)
-        f_out(0, 1)
         nc.scalar.copy(out=vec_cols[:], in_=vec_ps[:, 0 : 3 * PACK])
-        f_quantize(0, 0, 256)
+        permute_weight(W2)
+
+        widen(1, 0)
+        f_quantize(0, 0, HALF)
         widen(1, 1)
         widen(1, 2)
-        f_quantize(0, 256, 512)
+        f_quantize(0, HALF, CHUNK)
         widen(1, 3)
-        widen(2, 0)
-        widen(2, 1)
-        widen(2, 2)
-        widen(2, 3)
+        for pair in range(2):
+            v_first_pair(0, pair)
+        for j in range(PACK):
+            v_gelu(0, j, 0, HALF)
+        for half in range(2):
+            f_turn(1, half)
+            f_out(1, half)
+            v_first_pair(1, half)
+            for j in range(1) if half == 0 else range(1, PACK):
+                v_gelu(0, j, HALF, CHUNK)
+
+        for a in range(PACK):
+            widen(2, a)
         widen(3, 0)
-        first_matmul(0, 0)
-        first_matmul(0, 1)
-        first_matmul(0, 2)
-        first_matmul(0, 3)
-        f_turn(1, 0)
-        first_matmul(1, 0)
-        first_matmul(1, 1)
-        f_turn(1, 1)
-        first_matmul(1, 2)
-        first_matmul(1, 3)
-        v_gelu(0, 0, 0, 256)
-        v_gelu(0, 1, 0, 256)
-        v_gelu(0, 2, 0, 256)
-        v_gelu(0, 3, 0, 256)
-        f_out(1, 0)
-        v_gelu(0, 0, 256, 512)
-        f_out(1, 1)
-        v_gelu(0, 1, 256, 512)
-        v_gelu(0, 2, 256, 512)
-        v_gelu(0, 3, 256, 512)
-        f_turn(2, 0)
-        f_turn(2, 1)
         f_quantize(1)
-        widen(3, 1)
-        widen(3, 2)
-        widen(3, 3)
-        quantize(t_mx, t_grouped)
-        permute_weight(0)
-        f_out(2, 0)
-        f_out(2, 1)
-        v_matmul(1, 0, bank(2, "v_ps1_0")[:])
-        v_matmul(1, 1, bank(3, "v_ps1_1")[:])
+        for half in range(2):
+            f_turn(2, half)
+            f_out(2, half)
+        for a in range(1, PACK):
+            widen(3, a)
+        quantize(t_mx, 0, B * Q, t_grouped[:])
+        permute_weight(W1)
+        for j in range(2):
+            v_whole(1, j)
+        for j in range(2):
+            v_gelu(1, j)
         f_turn(3, 0)
-        v_matmul(1, 2, bank(4, "v_ps1_2")[:])
-        v_matmul(1, 3, bank(5, "v_ps1_3")[:])
+        f_out(3, 0)
+        for j in range(2, PACK):
+            v_whole(1, j)
+        v_gelu(1, 2)
         f_turn(3, 1)
+        f_out(3, 1)
+        v_gelu(1, 3)
+
         h_matmul(0)
         h_matmul(1)
         f_quantize(2)
-        y_gain(0, 0, 256)
-        v_gelu(1, 0)
-        v_gelu(1, 1)
-        f_out(3, 0)
-        v_gelu(1, 2)
-        f_out(3, 1)
-        v_gelu(1, 3)
-        v_matmul(2, 0, bank(2, "v_ps2_0")[:])
-        v_matmul(2, 1, bank(3, "v_ps2_1")[:])
-        v_matmul(2, 2, bank(4, "v_ps2_2")[:])
-        v_matmul(2, 3, bank(5, "v_ps2_3")[:])
+        y_gain(0, vec_cols, 0, HALF)
         f_quantize(3)
-        y_gain(0, 256, 512)
+        side_gain(0)
+        for j in range(2):
+            v_whole(2, j)
+        gain_ps = bank(1, "gain_ps", P, BF16)
+        nc.tensor.transpose(gain_ps[:], vec_rows[:], ident_bf[:])
+        for j in range(2, PACK):
+            v_whole(2, j)
+        for j in range(PACK):
+            v_gelu(2, j)
+        y_gain(0, gain_ps, HALF, CHUNK)
         h_out(0)
-        y_quantize(0)
         h_out(1)
-        y_gain(1, 0, 256)
-        quantize(h_mx, h_grouped, 0, 256)
-        y_gain(1, 256, 512)
-        v_gelu(2, 0)
-        v_gelu(2, 1)
-        v_gelu(2, 2)
-        v_gelu(2, 3)
-        v_matmul(3, 0, bank(2, "v_ps3_0")[:])
-        v_matmul(3, 1, bank(3, "v_ps3_1")[:])
-        v_matmul(3, 2, bank(4, "v_ps3_2")[:])
-        v_matmul(3, 3, bank(5, "v_ps3_3")[:])
-        h_matmul(2)
-        mask_matmul(0, 0, 0)
-        mask_matmul(0, 1, 1)
-        h_matmul(3)
+        for pair in range(2):
+            for j in range(2 * pair, 2 * pair + 2):
+                v_whole(3, j)
+            h_matmul(2 + pair)
+        for j in range(PACK):
+            v_gelu(3, j)
         h_out(2)
-        y_quantize(1)
+        y_quantize(0)
+        side_quantize(0)
+        h_quantize(0)
+        side_gain(1)
+        mask_matmul(0, 0, 0)
+        mask_matmul(0, 1, 2)
+
+        y_gain(2, gain_ps)
         h_out(3)
-        y_gain(2)
-        quantize(h_mx, h_grouped, 256, 512)
+        side_quantize(1)
         y_quantize(2)
-        v_gelu(3, 0)
-        v_gelu(3, 1)
-        v_gelu(3, 2)
-        v_gelu(3, 3)
-        ps_sigmoids(0, 0, (1,))
-        ps_sigmoids(0, 0, (0,))
-        ps_sigmoids(0, 1, (1,))
-        ps_sigmoids(0, 1, (0,))
-        mask_out(0, 0, False)
-        mask_out(0, 1, False)
-        mask_matmul(1, 0, 2)
-        mask_matmul(1, 1, 3)
-        mask_matmul(2, 0, 4)
-        mask_matmul(2, 1, 5)
-        y_gain(3)
-        ps_sigmoids(1, 0, (1,))
-        ps_sigmoids(1, 0, (0,))
-        ps_sigmoids(1, 1, (1,))
-        ps_sigmoids(1, 1, (0,))
-        ps_sigmoids(2, 0, (1,))
-        ps_sigmoids(2, 0, (0,))
-        ps_sigmoids(2, 1, (1,))
-        ps_sigmoids(2, 1, (0,))
-        mask_out(1, 0, True)
+        h_quantize(1)
+        for a in range(2):
+            sigmoid_sums(0, a)
+        mask_out(0, 0, on_scalar=True)
+        for c in (1, 2):
+            for a in range(2):
+                mask_matmul(c, a, 1 + 2 * c + a)
+        y_gain(3, gain_ps)
+        mask_out(0, 1)
         y_quantize(3)
-        mask_out(1, 1, True)
-        outer_recip(0, 2)
-        mask_out(2, 0, True)
+        mask_matmul(3, 0, 7)
+        mask_matmul(3, 1, 1)
+        for a in range(2):
+            sigmoid_sums(1, a)
+            mask_out(1, a)
+        outer_recip(0)
+        sigmoid_sums(2, 0)
+        mask_out(2, 0)
         ratio(0)
         ratio(1)
-        mask_matmul(3, 0, 6)
-        mask_matmul(3, 1, 7)
-        mask_out(3, 1, True)
-        mask_out(2, 1, True)
-        ps_sigmoids(3, 0, (1,))
-        ps_sigmoids(3, 0, (0,))
-        ps_sigmoids(3, 1, (1,))
-        ps_sigmoids(3, 1, (0,))
-        mask_out(3, 0, True)
-        outer_recip(2, 4)
+        sigmoid_sums(2, 1)
+        mask_out(3, 1)
+        mask_out(2, 1)
+        sigmoid_sums(3, 0)
+        mask_out(3, 0)
+        sigmoid_sums(3, 1)
+        outer_recip(1)
         ratio(2)
         ratio(3)
 

import math
from contextlib import ExitStack

import concourse.mybir as mybir
from concourse.masks import make_identity

B, Q, N, D, E = 2, 256, 1024, 512, 512
FLOPS = 2 * B * Q * D * E + 2 * B * N * D * E + 2 * B * Q * N * E

F32 = mybir.dt.float32
BF16 = mybir.dt.bfloat16
I32 = mybir.dt.int32
U32 = mybir.dt.uint32
U8 = mybir.dt.uint8
FP8 = mybir.dt.float8_e4m3fn
FP8X4 = mybir.dt.float8_e4m3fn_x4
FP4X4 = mybir.dt.float4_e2m1fn_x4
ACT = mybir.ActivationFunctionType
ALU = mybir.AluOpType

P = 128
PACK = 4
BANK = 512
CHUNK = 512
HALF = CHUNK // 2
CHUNKS = B * N // CHUNK
TILES = B * Q // P
RUN = 4
MASK_SCALE = 2.0 / math.sqrt(E)
W1, W2 = 0, 1
BIAS1, BIAS2, GAIN = 0, 1, 2
INNER, OUTER = 0, 1


def tile_hypertokenmaskheadsoftstability_w4_kernel(
    tc, t, w1_words, w1_scales, b1, f_bytes, f_scale, w2_words, w2_scales, b2, g, out_0, out_1
):
    nc = tc.nc
    with ExitStack() as ctx:
        sb = ctx.enter_context(tc.tile_pool(name="sb", bufs=1))
        ps = ctx.enter_context(tc.psum_pool(name="ps", bufs=1))
        ctx.enter_context(tc.manual_schedule())

        def sbuf(name, shape, dtype, tag=None):
            return sb.tile(shape, dtype, name=name, tag=tag or name, align_bytes=64)

        def bank(index, name, width=BANK, dtype=F32):
            return ps.tile([P, width], dtype, name=name, tag="bank%d" % index)

        warm_in = sbuf("warm_in", [P, 16], F32)
        warm_out = sbuf("warm_out", [P, 16], F32)
        nc.vector.memset(warm_in[:], 0.0)
        nc.scalar.activation(out=warm_out[:], in_=warm_in[:], func=ACT.Gelu_apprx_tanh)
        ident = sbuf("ident", [P, P], F32)
        make_identity(nc, ident[:])

        raw_scales = [sbuf("raw_scales%d" % w, [P, E], U8) for w in (W1, W2)]
        for w in (W1, W2):
            nc.vector.memset(raw_scales[w][:].bitcast(I32), 0)
        vec_rows = sbuf("vec_rows", [P, P], BF16)
        nc.vector.memset(vec_rows[:], 0.0)

        f_rows = f_bytes.rearrange("b (c r a) k -> (b c) r (a k)", r=P, a=PACK)
        fs_cols = sbuf("fs_cols", [P, PACK], F32)
        f_raw = [sbuf("f_raw%d" % c, [P, PACK * D], U8) for c in range(CHUNKS)]
        t_raw = [sbuf("t_raw%d" % b, [P, 2, D], BF16) for b in range(B)]
        raw_words = [sbuf("raw_words%d" % w, [P, 2 * E], U8) for w in (W1, W2)]

        def load_weight(w, words, scales):
            nc.sync.dma_start(out=raw_words[w][:].bitcast(I32), in_=words[0].bitcast(I32))
            for quad in range(4):
                nc.sync.dma_start(
                    out=raw_scales[w][32 * quad : 32 * quad + 4, :].bitcast(I32),
                    in_=scales[0, 4 * quad : 4 * quad + 4, :].bitcast(I32),
                )

        nc.sync.dma_start(out=fs_cols[:], in_=f_scale.rearrange("o u (p j) -> p (o u j)", j=PACK))
        nc.sync.dma_start(out=f_raw[0][:], in_=f_rows[0])
        for b in range(B):
            nc.sync.dma_start(out=t_raw[b][:], in_=t[b].rearrange("(a p) k -> p a k", p=P))
        load_weight(W2, w2_words, w2_scales)
        nc.sync.dma_start(out=f_raw[1][:], in_=f_rows[1])
        for v, vec in enumerate((b1, b2, g)):
            nc.sync.dma_start(
                out=vec_rows[PACK * v : PACK * (v + 1), :].rearrange("j (q i) -> j q i", i=8),
                in_=vec.rearrange("(q j i) -> j q i", j=PACK, i=8),
            )
        load_weight(W1, w1_words, w1_scales)
        for c in range(2, CHUNKS):
            nc.sync.dma_start(out=f_raw[c][:], in_=f_rows[c])

        ident_bf = sbuf("ident_bf", [P, P], BF16)
        nc.vector.tensor_copy(out=ident_bf[:], in_=ident[:])
        shift = sbuf("shift", [P, 2], F32)
        nc.vector.memset(shift[:, INNER : INNER + 1], -4.0)
        nc.vector.memset(shift[:, OUTER : OUTER + 1], 4.0)
        stab = sbuf("stab", [P, P], F32)
        nc.vector.memset(stab[:], 0.0)

        spread_ps = bank(2, "spread_ps")
        for j in range(PACK):
            nc.tensor.transpose(spread_ps[:, j * P : (j + 1) * P], fs_cols[:, j : j + 1].to_broadcast([P, P]), ident[:])
        fs_spread = sbuf("fs_spread", [P, D], F32)
        nc.scalar.copy(
            out=fs_spread[:].rearrange("x (p j) -> x p j", j=PACK),
            in_=spread_ps[:].rearrange("x (j p) -> x p j", j=PACK),
        )

        w_codes = [sbuf("w_codes%d" % w, [P, 2 * E], U8) for w in (W1, W2)]
        w_scales = [sbuf("w_scales%d" % w, [P, E], U8) for w in (W1, W2)]

        def permute_weight(w):
            for dst, src, words in ((w_codes, raw_words, 4), (w_scales, raw_scales, 2)):
                nc.vector.tensor_copy(
                    out=dst[w][:].bitcast(I32).rearrange("p (j q i) -> p j q i", j=PACK, i=words),
                    in_=src[w][:].bitcast(I32).rearrange("p (q j i) -> p j q i", j=PACK, i=words),
                )

        def weight_slice(w, j):
            return dict(
                lhsT=w_codes[w][:, 2 * P * j : 2 * P * (j + 1)].bitcast(FP4X4),
                lhsT_scale=w_scales[w][:, P * j : P * (j + 1)],
            )

        def mx_tiles(name):
            return sbuf(name + "_codes", [P, CHUNK], U32), sbuf(name + "_scales", [P, CHUNK], U8)

        def quantize(mx, lo, hi, grouped):
            nc.vector.quantize_mx(out=mx[0][:, lo:hi].bitcast(FP8X4), scales=mx[1][:, lo:hi], in_=grouped)

        def turn(index, name, rows):
            dst = bank(index, name)
            for slot in range(2):
                words = rows[slot].bitcast(F32)
                for u in range(2):
                    col = (2 * slot + u) * P
                    nc.tensor.transpose(dst[:, col : col + P], words[:, u : 2 * P : 2], ident[:])
            return dst

        def turned_out(grouped, half, src):
            words = grouped[:, PACK * HALF * half : PACK * HALF * (half + 1)].bitcast(F32)
            nc.scalar.copy(
                out=words.rearrange("p (a r u) -> p a r u", a=2, u=2),
                in_=src[:].rearrange("p (a u r) -> p a r u", a=2, u=2),
            )

        vec_cols = sbuf("vec_cols", [P, 3 * PACK], F32)
        f_wide = [[sbuf("f_wide%d_%d" % (c, a), [P, D], BF16) for a in range(PACK)] for c in range(CHUNKS)]
        f_grouped = [
            sbuf("f_grouped%d" % c, [P, PACK * CHUNK], BF16, "side0" if c == CHUNKS - 1 else None) for c in range(CHUNKS)
        ]
        t_grouped = sbuf("t_grouped", [P, PACK * B * Q], BF16)
        h_grouped = [sbuf("h_grouped%d" % b, [P, PACK * Q], BF16, "side1" if b == 0 else None) for b in range(B)]
        gelu = [sbuf("gelu%d" % c, [P, PACK, CHUNK], F32) for c in range(CHUNKS)]
        y_grouped = {c: sbuf("y_grouped%d" % c, [P, PACK * CHUNK], BF16) for c in (0, 2, 3)}
        f_mx = [mx_tiles("f%d" % c) for c in range(CHUNKS)]
        y_mx = [mx_tiles("y%d" % c) for c in range(CHUNKS)]
        t_mx, h_mx = mx_tiles("t"), mx_tiles("h")
        mask_sb = [sbuf("mask_sb%d" % tile, [P, N], F32) for tile in range(TILES)]
        sums = sbuf("sums", [P, 2, TILES, 2], F32)
        outer = sbuf("outer", [P, TILES], F32)
        recip = sbuf("recip", [P, TILES], F32)
        f_turned, v_ps, h_ps, mask_ps, y_side = {}, {}, {}, {}, {}

        def widen(c, a):
            nc.vector.tensor_tensor(
                out=f_wide[c][a][:], in0=f_raw[c][:, a * D : (a + 1) * D].bitcast(FP8), in1=fs_spread[:], op=ALU.mult
            )

        def f_turn(c, half):
            rows = [f_wide[c][2 * half + slot][:] for slot in range(2)]
            f_turned[c, half] = turn(half, "f_turned%d_%d" % (c, half), rows)

        def f_out(c, half):
            turned_out(f_grouped[c], half, f_turned[c, half])

        def f_quantize(c, lo=0, hi=CHUNK):
            quantize(f_mx[c], lo, hi, f_grouped[c][:, PACK * lo : PACK * hi])

        def v_matmul(c, j, dst, lo=0, hi=CHUNK):
            v_ps[c, j, lo] = dst
            nc.tensor.matmul_mx(
                out=dst, rhs=f_mx[c][0][:, lo:hi].bitcast(FP8X4), rhs_scale=f_mx[c][1][:, lo:hi],
                start=True, stop=True, **weight_slice(W2, j)
            )

        def v_whole(c, j):
            v_matmul(c, j, bank(2 + j, "v_ps%d_%d" % (c, j))[:])

        def v_first_pair(half, pair):
            dst = bank(2 + 2 * half + pair, "v_first%d_%d" % (half, pair))
            for slot in range(2):
                v_matmul(0, 2 * pair + slot, dst[:, HALF * slot : HALF * (slot + 1)], HALF * half, HALF * (half + 1))

        def v_gelu(c, j, lo=0, hi=CHUNK):
            col = PACK * BIAS2 + j
            nc.scalar.activation(
                out=gelu[c][:, j, lo:hi], in_=v_ps[c, j, lo], func=ACT.Gelu_apprx_tanh, bias=vec_cols[:, col : col + 1]
            )

        def gain(engine, dst, c, lo, hi, cols):
            gains = cols[:, PACK * GAIN : PACK * (GAIN + 1)].unsqueeze(1).unsqueeze(3)
            engine.tensor_tensor(
                out=dst.rearrange("p (c i j) -> p c j i", i=RUN, j=PACK),
                in0=gelu[c][:, :, lo:hi].rearrange("p j (c i) -> p c j i", i=RUN),
                in1=gains.to_broadcast([P, (hi - lo) // RUN, PACK, RUN]),
                op=ALU.mult,
            )

        def y_gain(c, cols, lo=0, hi=CHUNK):
            gain(nc.vector, y_grouped[c][:, PACK * lo : PACK * hi], c, lo, hi, cols)

        def y_quantize(c):
            quantize(y_mx[c], 0, CHUNK, y_grouped[c][:])

        def side_gain(half):
            y_side[half] = sbuf("y_side%d" % half, [P, PACK * HALF], BF16, "side%d" % half)
            gain(nc.gpsimd, y_side[half][:], 1, HALF * half, HALF * (half + 1), vec_cols)

        def side_quantize(half):
            quantize(y_mx[1], HALF * half, HALF * (half + 1), y_side[half][:])

        def h_matmul(tile):
            h_ps[tile] = bank(6 + tile % 2, "h_ps%d" % tile)
            cols = slice(tile * P, (tile + 1) * P)
            for j in range(PACK):
                nc.tensor.matmul_mx(
                    out=h_ps[tile][:, j * P : (j + 1) * P], rhs=t_mx[0][:, cols].bitcast(FP8X4), rhs_scale=t_mx[1][:, cols],
                    start=True, stop=True, **weight_slice(W1, j)
                )

        def h_out(tile):
            lo = PACK * P * (tile % 2)
            nc.vector.tensor_tensor(
                out=h_grouped[tile // 2][:, lo : lo + PACK * P].rearrange("p (r j) -> p r j", j=PACK),
                in0=h_ps[tile][:].rearrange("p (j r) -> p r j", j=PACK),
                in1=vec_cols[:, PACK * BIAS1 : PACK * (BIAS1 + 1)].unsqueeze(1).to_broadcast([P, P, PACK]),
                op=ALU.add,
            )

        def h_quantize(b):
            quantize(h_mx, Q * b, Q * (b + 1), h_grouped[b][:])

        def mask_matmul(c, a, index):
            mask_ps[c, a] = bank(index, "mask_ps%d_%d" % (c, a))
            tile = c // 2 * 2 + a
            cols = slice(tile * P, (tile + 1) * P)
            nc.tensor.matmul_mx(
                out=mask_ps[c, a][:], lhsT=h_mx[0][:, cols].bitcast(FP8X4), lhsT_scale=h_mx[1][:, cols],
                rhs=y_mx[c][0][:].bitcast(FP8X4), rhs_scale=y_mx[c][1][:], start=True, stop=True,
            )

        def mask_out(c, a, on_scalar=False):
            cols = slice(c % 2 * CHUNK, (c % 2 + 1) * CHUNK)
            rows = mask_sb[c // 2 * 2 + a][:, cols]
            dst = rows.rearrange("p (r a) -> p r a", a=PACK)
            src = mask_ps[c, a][:].rearrange("p (a r) -> p r a", a=PACK)
            if on_scalar:
                nc.scalar.activation(out=dst, in_=src, func=ACT.Copy, scale=MASK_SCALE)
            else:
                nc.vector.tensor_scalar(out=dst, in0=src, scalar1=MASK_SCALE, scalar2=None, op0=ALU.mult)
            nc.sync.dma_start(out=out_0[c // 2, a * P : (a + 1) * P, cols], in_=rows)

        def sigmoid_sums(c, a):
            tile = c // 2 * 2 + a
            for side in (OUTER, INNER):
                values = sbuf("sigmoid%d_%d_%d" % (c, a, side), [P, CHUNK], BF16)
                nc.scalar.activation(
                    out=values[:], in_=mask_ps[c, a][:], func=ACT.Sigmoid, scale=4.0 * MASK_SCALE,
                    bias=shift[:, side : side + 1], accum_out=sums[:, side, tile, c % 2 : c % 2 + 1],
                )

        def outer_recip(b):
            tiles = slice(2 * b, 2 * b + 2)
            nc.vector.tensor_tensor(out=outer[:, tiles], in0=sums[:, OUTER, tiles, 0], in1=sums[:, OUTER, tiles, 1], op=ALU.add)
            nc.vector.reciprocal(out=recip[:, tiles], in_=outer[:, tiles])

        def ratio(tile):
            nc.vector.scalar_tensor_tensor(
                out=stab[:, 32 * tile : 32 * tile + 1], in0=sums[:, INNER, tile, 0:1], scalar=sums[:, INNER, tile, 1:2],
                in1=recip[:, tile : tile + 1], op0=ALU.add, op1=ALU.mult,
            )

        for a in range(PACK):
            widen(0, a)
        for b in range(B):
            turned_out(t_grouped, b, turn(6 + b, "t_turned%d" % b, [t_raw[b][:, slot, :] for slot in range(2)]))
        for half in range(2):
            f_turn(0, half)
            f_out(0, half)
        vec_ps = bank(5, "vec_ps", P, BF16)
        nc.tensor.transpose(vec_ps[:], vec_rows[:], ident_bf[:])
        nc.scalar.copy(out=vec_cols[:], in_=vec_ps[:, 0 : 3 * PACK])
        permute_weight(W2)

        widen(1, 0)
        f_quantize(0, 0, HALF)
        widen(1, 1)
        widen(1, 2)
        f_quantize(0, HALF, CHUNK)
        widen(1, 3)
        for pair in range(2):
            v_first_pair(0, pair)
        for j in range(PACK):
            v_gelu(0, j, 0, HALF)
        for half in range(2):
            f_turn(1, half)
            f_out(1, half)
            v_first_pair(1, half)
            for j in range(1) if half == 0 else range(1, PACK):
                v_gelu(0, j, HALF, CHUNK)

        for a in range(PACK):
            widen(2, a)
        widen(3, 0)
        f_quantize(1)
        for half in range(2):
            f_turn(2, half)
            f_out(2, half)
        for a in range(1, PACK):
            widen(3, a)
        quantize(t_mx, 0, B * Q, t_grouped[:])
        permute_weight(W1)
        for j in range(2):
            v_whole(1, j)
        for j in range(2):
            v_gelu(1, j)
        f_turn(3, 0)
        f_out(3, 0)
        for j in range(2, PACK):
            v_whole(1, j)
        v_gelu(1, 2)
        f_turn(3, 1)
        f_out(3, 1)
        v_gelu(1, 3)

        h_matmul(0)
        h_matmul(1)
        f_quantize(2)
        y_gain(0, vec_cols, 0, HALF)
        f_quantize(3)
        side_gain(0)
        for j in range(2):
            v_whole(2, j)
        gain_ps = bank(1, "gain_ps", P, BF16)
        nc.tensor.transpose(gain_ps[:], vec_rows[:], ident_bf[:])
        for j in range(2, PACK):
            v_whole(2, j)
        for j in range(PACK):
            v_gelu(2, j)
        y_gain(0, gain_ps, HALF, CHUNK)
        h_out(0)
        h_out(1)
        for pair in range(2):
            for j in range(2 * pair, 2 * pair + 2):
                v_whole(3, j)
            h_matmul(2 + pair)
        for j in range(PACK):
            v_gelu(3, j)
        h_out(2)
        y_quantize(0)
        side_quantize(0)
        h_quantize(0)
        side_gain(1)
        mask_matmul(0, 0, 0)
        mask_matmul(0, 1, 2)

        y_gain(2, gain_ps)
        h_out(3)
        side_quantize(1)
        y_quantize(2)
        h_quantize(1)
        for a in range(2):
            sigmoid_sums(0, a)
        mask_out(0, 0, on_scalar=True)
        for c in (1, 2):
            for a in range(2):
                mask_matmul(c, a, 1 + 2 * c + a)
        y_gain(3, gain_ps)
        mask_out(0, 1)
        y_quantize(3)
        mask_matmul(3, 0, 7)
        mask_matmul(3, 1, 1)
        for a in range(2):
            sigmoid_sums(1, a)
            mask_out(1, a)
        outer_recip(0)
        sigmoid_sums(2, 0)
        mask_out(2, 0)
        ratio(0)
        ratio(1)
        sigmoid_sums(2, 1)
        mask_out(3, 1)
        mask_out(2, 1)
        sigmoid_sums(3, 0)
        mask_out(3, 0)
        sigmoid_sums(3, 1)
        outer_recip(1)
        ratio(2)
        ratio(3)

        stab_turned = sbuf("stab_turned", [P, P], F32)
        nc.vector.transpose(out=stab_turned[:], in_=stab[:])
        nc.sync.dma_start(
            out=out_1.rearrange("b (a s i) -> s (b a) i", a=2, i=32),
            in_=stab_turned[0:P:32, :].rearrange("s (j i) -> s j i", i=32),
        )
